import numpy as np
import ml_dtypes


def mxq(x, axis, fmt="e4m3"):
    dtype, down = {"e4m3": (ml_dtypes.float8_e4m3fn, 7), "e5m2": (ml_dtypes.float8_e5m2, 14)}[fmt]
    v = np.moveaxis(np.asarray(x, np.float32).astype(ml_dtypes.bfloat16).astype(np.float64), axis, -1)
    blocks = v.reshape(v.shape[:-1] + (-1, 32))
    amax = np.abs(blocks).max(-1, keepdims=True)
    byte = np.maximum(np.where(amax > 0, np.frexp(amax)[1] - 1 + 127, 0) - down, 1)
    scale = np.exp2(byte - 127.0)
    codes = (blocks / scale).astype(np.float32).astype(dtype).astype(np.float64)
    return np.moveaxis((codes * scale).reshape(v.shape), -1, axis)


WIDE = False


def mx_kscale(k):
    if not WIDE:
        return np.ones(k)
    levels = np.array([30, -30])
    if k % 512:
        return np.exp2(np.random.permutation(np.resize(levels, k // 32))).repeat(32)
    a = np.empty((k // 512, 16))
    for p in range(k // 512):
        a[p, :8] = np.random.permutation(np.resize(levels, 8))
        for g in range(8):
            far = levels[np.abs(levels - a[p, g]) >= 10]
            a[p, g + 8] = far[np.random.randint(len(far))]
    return np.exp2(a.ravel()).repeat(32)


def f64(x):
    return np.asarray(x).astype(np.float64)


def striped(idx):
    return np.tile(np.asarray(idx).reshape(-1, 16).T, (8, 1)).astype(np.uint16)


def unstriped(offs):
    return offs[:16].T.reshape(-1).astype(np.int64)


E2M1 = np.array([0.0, 0.5, 1.0, 1.5, 2.0, 3.0, 4.0, 6.0, -0.0, -0.5, -1.0, -1.5, -2.0, -3.0, -4.0, -6.0])


def pack_weight(w, fmt):
    k, n = w.shape
    w = f64(np.asarray(w, np.float32).astype(ml_dtypes.bfloat16)).reshape(k // 32, 32, n)
    amax = np.abs(w).max(1)
    if fmt in ("e4m3", "e5m2"):
        byte = np.frexp(amax)[1] - 1 + 127 - (7 if fmt == "e4m3" else 14)
    else:
        mant, ex = np.frexp(amax / 6.0)
        byte = np.where(mant > 0.5, ex, ex - 1) + 127
    byte = np.clip(np.where(amax > 0, byte, 1), 1, 254)
    scaled = (w * np.exp2(127.0 - byte)[:, None, :]).reshape(k, n).astype(np.float32)
    by_word = np.ascontiguousarray(scaled.reshape(k // 512, 128, 4, n).transpose(0, 1, 3, 2))
    if fmt in ("e4m3", "e5m2"):
        words = by_word.astype(ml_dtypes.float8_e4m3fn if fmt == "e4m3" else ml_dtypes.float8_e5m2).view(np.uint8)
    else:
        c = by_word.astype(ml_dtypes.float4_e2m1fn).view(np.uint8) & 0xF
        words = (c[..., 0::2] | (c[..., 1::2] << 4)).reshape(k // 512, 128, 2 * n)
    return np.ascontiguousarray(words), np.ascontiguousarray(byte.astype(np.uint8).reshape(k // 512, 16, n))


def unpack_weight(words, scales, fmt):
    g, _, n = scales.shape
    words = np.ascontiguousarray(words).reshape(g, 128, n, -1)
    if fmt in ("e4m3", "e5m2"):
        vals = words.view(ml_dtypes.float8_e4m3fn if fmt == "e4m3" else ml_dtypes.float8_e5m2).astype(np.float64)
    else:
        nib = np.empty((g, 128, n, 4), np.uint8)
        nib[..., 0::2] = words & 0xF
        nib[..., 1::2] = words >> 4
        vals = E2M1[nib]
    vals = vals * np.repeat(np.exp2(scales.astype(np.float64) - 127.0), 8, axis=1)[..., None]
    return vals.transpose(0, 1, 3, 2).reshape(g * 512, n)


def sigmoid(v):
    return 1.0 / (1.0 + np.exp(-v))


def sgn(shape):
    return np.random.uniform(0.5, 2.0, shape) * np.where(np.random.standard_normal(shape) < 0, -1.0, 1.0)


K, T, J, R, F, Z, C, O, N = 512, 1024, 256, 512, 512, 1024, 512, 256, 256


def setup_inputs():
    n = np.random.standard_normal
    idx = np.random.permutation(T)[:J]
    idx2 = np.random.permutation(Z)[:J]
    idx3 = np.random.permutation(C)[:J]
    idx4 = np.random.permutation(C)[:C]
    idx5 = np.random.permutation(C)[:C]
    idx6 = np.random.permutation(C)[:O]
    idx7 = np.random.permutation(T)[:O]
    fk = mx_kscale(K)
    ff = mx_kscale(F)
    fr = mx_kscale(R)
    xtp = pack_weight(n((K, T)) / fk[:, None], "e4m3")
    xop = pack_weight(n((F, Z)) / ff[:, None], "e2m1")
    wp = pack_weight(n((K, R)) * 1 / np.sqrt(K) * fk[:, None], "e2m1")
    w0p = pack_weight(n((F, R)) * 1 / np.sqrt(F) * ff[:, None], "e5m2")
    wbp = pack_weight(n((R, N)) * 1 / np.sqrt(R) / fr[:, None], "e5m2")
    wsp = pack_weight(n((K, N)) * 1 / np.sqrt(K) * fk[:, None], "e5m2")
    return {
        "xt_words": xtp[0],
        "xt_scales": xtp[1],
        "xo_words": xop[0],
        "xo_scales": xop[1],
        "w_words": wp[0],
        "w_scales": wp[1],
        "w0_words": w0p[0],
        "w0_scales": w0p[1],
        "sa": (sgn((R, 1))).astype(np.float32),
        "sb": (np.random.uniform(0.5, 1.6, (R, 1)) * fr[:, None]).astype(np.float32),
        "sg": (sgn((R, 1))).astype(np.float32),
        "bg": (np.random.uniform(-2.0, 2.0, (R, 1))).astype(np.float32),
        "wb_words": wbp[0],
        "wb_scales": wbp[1],
        "ws_words": wsp[0],
        "ws_scales": wsp[1],
        "offs": striped(idx),
        "offs2": striped(idx2),
        "offs3": striped(idx3),
        "offs4": striped(idx4),
        "offs5": striped(idx5),
        "offs6": striped(idx6),
        "offs7": striped(idx7),
    }


def reference(xt_words, xt_scales, xo_words, xo_scales, w_words, w_scales, w0_words, w0_scales, sa, sb, sg, bg, wb_words, wb_scales, ws_words, ws_scales, offs, offs2, offs3, offs4, offs5, offs6, offs7):
    idx = unstriped(offs)
    idx2 = unstriped(offs2)
    idx3 = unstriped(offs3)
    idx4 = unstriped(offs4)
    idx5 = unstriped(offs5)
    idx6 = unstriped(offs6)
    idx7 = unstriped(offs7)
    xtu = unpack_weight(xt_words, xt_scales, "e4m3")
    xou = unpack_weight(xo_words, xo_scales, "e2m1")
    wu = unpack_weight(w_words, w_scales, "e2m1")
    w0u = unpack_weight(w0_words, w0_scales, "e5m2")
    wbu = unpack_weight(wb_words, wb_scales, "e5m2")
    wsu = unpack_weight(ws_words, ws_scales, "e5m2")
    xtidxg = xtu[:, idx]
    xoidx2g = xou[:, idx2]
    a = wu.T @ xtidxg + w0u.T @ xoidx2g
    pw = np.zeros((R, C))
    pw[:, idx3] = a
    pg = np.maximum(pw, pw[:, idx4] * f64(sa) * sigmoid(pw[:, idx5] * f64(sg) + f64(bg)))
    hid = pg[:, idx6] * f64(sb)
    hidq = mxq(hid, 0, "e4m3")
    xtidx7g = xtu[:, idx7]
    y = wbu.T @ hidq + wsu.T @ xtidx7g
    return y

@@ -1,0 +1,231 @@
+from contextlib import ExitStack
+
+import concourse.mybir as mybir
+
+F32 = mybir.dt.float32
+BF16 = mybir.dt.bfloat16
+I32 = mybir.dt.int32
+U32 = mybir.dt.uint32
+U16 = mybir.dt.uint16
+U8 = mybir.dt.uint8
+E4M3 = mybir.dt.float8_e4m3fn_x4
+E5M2 = mybir.dt.float8_e5m2_x4
+E2M1 = mybir.dt.float4_e2m1fn_x4
+ACT = mybir.ActivationFunctionType
+ALU = mybir.AluOpType
+
+P = 128
+PACK = 4
+T, J, R, Z, C, O, N = 1024, 256, 512, 1024, 512, 256, 256
+FLOPS = 2 * 512 * (2 * R * J + 2 * N * O)
+
+
+def tile_list_gatedladder_bank_further_plain_kernel(
+    tc, xt_words, xt_scales, xo_words, xo_scales, w_words, w_scales, w0_words, w0_scales,
+    sa, sb, sg, bg, wb_words, wb_scales, ws_words, ws_scales,
+    offs, offs2, offs3, offs4, offs5, offs6, offs7, out,
+):
+    nc = tc.nc
+    with ExitStack() as ctx:
+        keep = ctx.enter_context(tc.tile_pool(name="keep", bufs=1))
+        reuse = ctx.enter_context(tc.tile_pool(name="reuse", bufs=1))
+        psum = ctx.enter_context(tc.psum_pool(name="psum", bufs=1))
+
+        def sb_tile(shape, dtype, name):
+            return keep.tile(shape, dtype, name=name, align_bytes=64)
+
+        def load_list(src, name):
+            tile = sb_tile(list(src.shape), U16, name)
+            nc.sync.dma_start(tile[:], src)
+            return tile
+
+        def load_words(src, dtype, cols, name):
+            tile = sb_tile([P, cols], dtype, name)
+            flat = src[0] if len(src.shape) == 3 else src[0].rearrange("p c t -> p (c t)")
+            nc.sync.dma_start(tile[:].bitcast(I32), flat.bitcast(I32))
+            return tile
+
+        def load_per_row(src, name):
+            tile = sb_tile([P, PACK], F32, name)
+            nc.sync.dma_start(tile[:], src.rearrange("(p t) o -> p (t o)", t=PACK))
+            return tile
+
+        def stage_rows(dst, src):
+            nc.sync.dma_start(dst.bitcast(I32), src[0].bitcast(I32).rearrange("(q r) c -> r q c", r=4))
+
+        xt_st = sb_tile([4, 4, T], U8, "xt_st")
+        xo_st = sb_tile([4, 4, Z], U8, "xo_st")
+        w_s = reuse.tile([P, 2, 2 * R], U8, name="w_s", align_bytes=64, offset=0)
+        nc.vector.memset(w_s[:].bitcast(I32), 0)
+        stage_rows(xt_st[:], xt_scales)
+        stage_rows(xo_st[:], xo_scales)
+
+        l1 = load_list(offs, "l1")
+        l2 = load_list(offs2, "l2")
+        xt_w = load_words(xt_words, U32, T, "xt_w")
+        xo_w = load_words(xo_words, U16, Z, "xo_w")
+        w_raw = load_words(w_words, U16, R, "w_raw")
+        w0_raw = load_words(w0_words, U32, R, "w0_raw")
+        for src, cols in ((w_scales, slice(0, R)), (w0_scales, slice(R, 2 * R))):
+            rows = src[0].bitcast(I32).rearrange("(h q r) c -> q r h c", h=2, q=2)
+            for q in range(2):
+                nc.sync.dma_start(w_s[32 * q : 32 * q + 4, :, cols].bitcast(I32), rows[q])
+        l3 = load_list(offs3, "l3")
+        l5 = load_list(offs5, "l5")
+        sg_t = load_per_row(sg, "sg_t")
+        bg_t = load_per_row(bg, "bg_t")
+        l4 = load_list(offs4, "l4")
+        sa_t = load_per_row(sa, "sa_t")
+        l7 = load_list(offs7, "l7")
+        l6 = load_list(offs6, "l6")
+        sb_t = load_per_row(sb, "sb_t")
+        ws_w = load_words(ws_words, U32, N, "ws_w")
+        wb_w = load_words(wb_words, U32, N, "wb_w")
+
+        xt_s = sb_tile([P, T], U8, "xt_s")
+        xo_s = sb_tile([P, Z], U8, "xo_s")
+        for plane in (xt_s, xo_s):
+            nc.vector.memset(plane[:].bitcast(I32), 0)
+        pw = [sb_tile([P, C], F32, "pw%d" % t) for t in range(PACK)]
+        for t in range(PACK):
+            nc.vector.memset(pw[t][:], 0.0)
+        ws_s = sb_tile([P, N], U8, "ws_s")
+        wb_s = sb_tile([P, N], U8, "wb_s")
+        for plane, src in ((ws_s, ws_scales), (wb_s, wb_scales)):
+            nc.vector.memset(plane[:].bitcast(I32), 0)
+            for q in range(4):
+                nc.sync.dma_start(plane[32 * q : 32 * q + 4, :].bitcast(I32), src[0, 4 * q : 4 * q + 4, :].bitcast(I32))
+
+        for q in range(4):
+            for plane, staged in ((xt_s, xt_st), (xo_s, xo_st)):
+                nc.vector.tensor_copy(plane[32 * q : 32 * q + 4, :].bitcast(I32), staged[:, q, :].bitcast(I32))
+        w_sraw = w_s[:, 0, :]
+
+        def deal(copy, src, cols, dtype, line, name):
+            first = sb_tile([P, cols], dtype, name + "0")
+            rest = sb_tile([P, PACK - 1, cols], dtype, name + "r")
+            by_t = src.rearrange("p (h l t) -> p h t l", l=line, t=PACK)
+            steps = [
+                lambda: copy(first[:].rearrange("p (h l) -> p h l", l=line), by_t[:, :, 0, :]),
+                lambda: copy(rest[:].rearrange("p t (h l) -> p h t l", l=line), by_t[:, :, 1:PACK, :]),
+            ]
+            return [first[:]] + [rest[:, t, :] for t in range(PACK - 1)], steps
+
+        w_sd, deal_s = deal(nc.vector.tensor_copy, w_sraw, 2 * P, U8, 16, "w_sd")
+        w_d, deal_w = deal(nc.scalar.copy, w_raw[:], P, U16, 8, "w_d")
+        w0_d, deal_w0 = deal(nc.scalar.copy, w0_raw[:], P, U32, 4, "w0_d")
+
+        def gather(src, lst, dtype, name, offset):
+            tile = reuse.tile([P, J], dtype, name=name, align_bytes=64, offset=offset)
+            nc.vector.tensor_copy(tile[:], src[:].indirect(lst[:]))
+            return tile
+
+        HJ = J // 2
+        sorts = (("xt_gs", U8, xt_s, l1, 0), ("xo_gs", U8, xo_s, l2, 128), ("xt_gw", U32, xt_w, l1, 512), ("xo_gw", U16, xo_w, l2, 256))
+
+        def gather_half(h):
+            got = {}
+            for name, dtype, src, lst, offset in sorts:
+                if h == 0:
+                    dst = sb_tile([P, HJ], dtype, name + "0")
+                else:
+                    dst = reuse.tile([P, HJ], dtype, name=name + "1", align_bytes=64, offset=offset)
+                nc.vector.tensor_copy(dst[:], src[:].indirect(lst[:, h * HJ // 16 : (h + 1) * HJ // 16]))
+                got[name] = dst
+            return got
+
+        def first_stage(t, got, acc):
+            nc.tensor.matmul_mx(
+                out=acc, lhsT=w_d[t].bitcast(E2M1), lhsT_scale=w_sd[t][:, 0:P],
+                rhs=got["xt_gw"][:].bitcast(E4M3), rhs_scale=got["xt_gs"][:], start=True, stop=False,
+            )
+            nc.tensor.matmul_mx(
+                out=acc, lhsT=w0_d[t].bitcast(E5M2), lhsT_scale=w_sd[t][:, P : 2 * P],
+                rhs=got["xo_gw"][:].bitcast(E2M1), rhs_scale=got["xo_gs"][:], start=False, stop=True,
+            )
+
+        def board_half(h, got):
+            acc = psum.tile([P, HJ], F32, name="acc0%d" % h, tag="b0%d" % h)
+            first_stage(0, got, acc[:])
+            a_sb = sb_tile([P, HJ], F32, "a_sb0%d" % h)
+            nc.scalar.copy(a_sb[:], acc[:])
+            nc.scalar.activation(pw[0][:].indirect(l3[:, h * HJ // 16 : (h + 1) * HJ // 16]), a_sb[:], ACT.Copy)
+
+        deal_w[0]()
+        deal_w0[0]()
+        half0 = gather_half(0)
+        nc.vector.tensor_copy(w_s[64:P, 0, :].bitcast(I32), w_s[0:64, 1, :].bitcast(I32))
+        deal_s[0]()
+        board_half(0, half0)
+        deal_w[1]()
+        deal_w0[1]()
+        deal_s[1]()
+        half1 = gather_half(1)
+        board_half(1, half1)
+        for t in range(1, PACK):
+            acc = psum.tile([P, J], F32, name="acc%d" % t, tag="b%d" % t)
+            first_stage(t, half0, acc[:, 0:HJ])
+            first_stage(t, half1, acc[:, HJ:J])
+            a_sb = sb_tile([P, J], F32, "a_sb%d" % t)
+            nc.vector.tensor_copy(a_sb[:], acc[:])
+            nc.vector.tensor_copy(pw[t][:].indirect(l3[:]), a_sb[:])
+
+        x7_gw = gather(xt_w, l7, U32, "x7_gw", 1792)
+        x7_gs = gather(xt_s, l7, U8, "x7_gs", 1024)
+
+        HO = O // 2
+        ys = [[psum.tile([P, HO], F32, name="y%d_%d" % (h, b), tag=("y0", "y1", "y2", "b00")[2 * h + b]) for b in range(2)] for h in range(2)]
+        for h in range(2):
+            for b in range(2):
+                nc.tensor.matmul_mx(
+                    out=ys[h][b][:], lhsT=ws_w[:, b * P : (b + 1) * P].bitcast(E5M2), lhsT_scale=ws_s[:, b * P : (b + 1) * P],
+                    rhs=x7_gw[:, h * HO : (h + 1) * HO].bitcast(E4M3), rhs_scale=x7_gs[:, h * HO : (h + 1) * HO],
+                    start=True, stop=False,
+                )
+
+        HC = C // 2
+        pg = [sb_tile([P, C], F32, "pg%d" % t) for t in range(PACK)]
+        for t in range(PACK):
+            gate = sb_tile([P, C], F32, "gate%d" % t)
+            pick = sb_tile([P, C], F32, "pick%d" % t)
+            prod = sb_tile([P, C], F32, "prod%d" % t)
+            for h in range(2):
+                cols = slice(h * HC, (h + 1) * HC)
+                lcols = slice(h * HC // 16, (h + 1) * HC // 16)
+                nc.scalar.activation(gate[:, cols], pw[t][:].indirect(l5[:, lcols]), ACT.Sigmoid,
+                                     bias=bg_t[:, t : t + 1], scale=sg_t[:, t : t + 1])
+                nc.scalar.activation(pick[:, cols], pw[t][:].indirect(l4[:, lcols]), ACT.Copy, scale=sa_t[:, t : t + 1])
+            for h in range(2):
+                cols = slice(h * HC, (h + 1) * HC)
+                nc.vector.tensor_tensor(prod[:, cols], pick[:, cols], gate[:, cols], ALU.mult)
+            for h in range(2):
+                cols = slice(h * HC, (h + 1) * HC)
+                nc.vector.tensor_tensor(pg[t][:, cols], pw[t][:, cols], prod[:, cols], ALU.max)
+
+        hid = [sb_tile([P, PACK, HO], F32, "hid%d" % h) for h in range(2)]
+        for h in range(2):
+            for t in range(PACK):
+                lcols = slice(h * HO // 16, (h + 1) * HO // 16)
+                nc.scalar.activation(hid[h][:, t, :], pg[t][:].indirect(l6[:, lcols]), ACT.Copy, scale=sb_t[:, t : t + 1])
+
+        woven = [sb_tile([P, HO, PACK], BF16, "woven%d" % h) for h in range(2)]
+        hq = [sb_tile([P, HO], U32, "hq%d" % h) for h in range(2)]
+        hs = [sb_tile([P, HO], U8, "hs%d" % h) for h in range(2)]
+        for h in range(2):
+            nc.vector.tensor_copy(
+                woven[h][:].rearrange("p (c i) t -> p c t i", i=4),
+                hid[h][:].rearrange("p t (c i) -> p c t i", i=4),
+            )
+        for h in range(2):
+            nc.vector.quantize_mx(out=hq[h][:].bitcast(E4M3), scales=hs[h][:], in_=woven[h][:].rearrange("p o t -> p (o t)"))
+        out_v = out.rearrange("(b p) o -> p b o", p=P)
+        for h in range(2):
+            res = sb_tile([P, 2, HO], F32, "res%d" % h)
+            for b in range(2):
+                nc.tensor.matmul_mx(
+                    out=ys[h][b][:], lhsT=wb_w[:, b * P : (b + 1) * P].bitcast(E5M2), lhsT_scale=wb_s[:, b * P : (b + 1) * P],
+                    rhs=hq[h][:].bitcast(E4M3), rhs_scale=hs[h][:], start=False, stop=True,
+                )
+            nc.scalar.copy(res[:, 0, :], ys[h][0][:])
+            nc.vector.tensor_copy(res[:, 1, :], ys[h][1][:])
+            nc.sync.dma_start(out_v[:, :, h * HO : (h + 1) * HO], res[:])

@@ -60,6 +60,10 @@ def tile_list_gatedladder_bank_further_plain_kernel(
         stage_rows(xt_st[:], xt_scales)
         stage_rows(xo_st[:], xo_scales)
 
+        warm_in = sb_tile([P, 1], F32, "warm_in")
+        warm_out = sb_tile([P, 1], F32, "warm_out")
+        nc.gpsimd.memset(warm_in[:], 0.0)
+        nc.scalar.activation(warm_out[:], warm_in[:], ACT.Sigmoid)
         l1 = load_list(offs, "l1")
         l2 = load_list(offs2, "l2")
         xt_w = load_words(xt_words, U32, T, "xt_w")

from contextlib import ExitStack

import concourse.mybir as mybir

F32 = mybir.dt.float32
BF16 = mybir.dt.bfloat16
I32 = mybir.dt.int32
U32 = mybir.dt.uint32
U16 = mybir.dt.uint16
U8 = mybir.dt.uint8
E4M3 = mybir.dt.float8_e4m3fn_x4
E5M2 = mybir.dt.float8_e5m2_x4
E2M1 = mybir.dt.float4_e2m1fn_x4
ACT = mybir.ActivationFunctionType
ALU = mybir.AluOpType

P = 128
PACK = 4
T, J, R, Z, C, O, N = 1024, 256, 512, 1024, 512, 256, 256
FLOPS = 2 * 512 * (2 * R * J + 2 * N * O)


def tile_list_gatedladder_bank_further_plain_kernel(
    tc, xt_words, xt_scales, xo_words, xo_scales, w_words, w_scales, w0_words, w0_scales,
    sa, sb, sg, bg, wb_words, wb_scales, ws_words, ws_scales,
    offs, offs2, offs3, offs4, offs5, offs6, offs7, out,
):
    nc = tc.nc
    with ExitStack() as ctx:
        keep = ctx.enter_context(tc.tile_pool(name="keep", bufs=1))
        reuse = ctx.enter_context(tc.tile_pool(name="reuse", bufs=1))
        psum = ctx.enter_context(tc.psum_pool(name="psum", bufs=1))

        def sb_tile(shape, dtype, name):
            return keep.tile(shape, dtype, name=name, align_bytes=64)

        def load_list(src, name):
            tile = sb_tile(list(src.shape), U16, name)
            nc.sync.dma_start(tile[:], src)
            return tile

        def load_words(src, dtype, cols, name):
            tile = sb_tile([P, cols], dtype, name)
            flat = src[0] if len(src.shape) == 3 else src[0].rearrange("p c t -> p (c t)")
            nc.sync.dma_start(tile[:].bitcast(I32), flat.bitcast(I32))
            return tile

        def load_per_row(src, name):
            tile = sb_tile([P, PACK], F32, name)
            nc.sync.dma_start(tile[:], src.rearrange("(p t) o -> p (t o)", t=PACK))
            return tile

        def stage_rows(dst, src):
            nc.sync.dma_start(dst.bitcast(I32), src[0].bitcast(I32).rearrange("(q r) c -> r q c", r=4))

        xt_st = sb_tile([4, 4, T], U8, "xt_st")
        xo_st = sb_tile([4, 4, Z], U8, "xo_st")
        w_s = reuse.tile([P, 2, 2 * R], U8, name="w_s", align_bytes=64, offset=0)
        nc.vector.memset(w_s[:].bitcast(I32), 0)
        stage_rows(xt_st[:], xt_scales)
        stage_rows(xo_st[:], xo_scales)

        warm_in = sb_tile([P, 1], F32, "warm_in")
        warm_out = sb_tile([P, 1], F32, "warm_out")
        nc.gpsimd.memset(warm_in[:], 0.0)
        nc.scalar.activation(warm_out[:], warm_in[:], ACT.Sigmoid)
        l1 = load_list(offs, "l1")
        l2 = load_list(offs2, "l2")
        xt_w = load_words(xt_words, U32, T, "xt_w")
        xo_w = load_words(xo_words, U16, Z, "xo_w")
        w_raw = load_words(w_words, U16, R, "w_raw")
        w0_raw = load_words(w0_words, U32, R, "w0_raw")
        for src, cols in ((w_scales, slice(0, R)), (w0_scales, slice(R, 2 * R))):
            rows = src[0].bitcast(I32).rearrange("(h q r) c -> q r h c", h=2, q=2)
            for q in range(2):
                nc.sync.dma_start(w_s[32 * q : 32 * q + 4, :, cols].bitcast(I32), rows[q])
        l3 = load_list(offs3, "l3")
        l5 = load_list(offs5, "l5")
        sg_t = load_per_row(sg, "sg_t")
        bg_t = load_per_row(bg, "bg_t")
        l4 = load_list(offs4, "l4")
        sa_t = load_per_row(sa, "sa_t")
        l7 = load_list(offs7, "l7")
        l6 = load_list(offs6, "l6")
        sb_t = load_per_row(sb, "sb_t")
        ws_w = load_words(ws_words, U32, N, "ws_w")
        wb_w = load_words(wb_words, U32, N, "wb_w")

        xt_s = sb_tile([P, T], U8, "xt_s")
        xo_s = sb_tile([P, Z], U8, "xo_s")
        for plane in (xt_s, xo_s):
            nc.vector.memset(plane[:].bitcast(I32), 0)
        pw = [sb_tile([P, C], F32, "pw%d" % t) for t in range(PACK)]
        for t in range(PACK):
            nc.vector.memset(pw[t][:], 0.0)
        ws_s = sb_tile([P, N], U8, "ws_s")
        wb_s = sb_tile([P, N], U8, "wb_s")
        for plane, src in ((ws_s, ws_scales), (wb_s, wb_scales)):
            nc.vector.memset(plane[:].bitcast(I32), 0)
            for q in range(4):
                nc.sync.dma_start(plane[32 * q : 32 * q + 4, :].bitcast(I32), src[0, 4 * q : 4 * q + 4, :].bitcast(I32))

        for q in range(4):
            for plane, staged in ((xt_s, xt_st), (xo_s, xo_st)):
                nc.vector.tensor_copy(plane[32 * q : 32 * q + 4, :].bitcast(I32), staged[:, q, :].bitcast(I32))
        w_sraw = w_s[:, 0, :]

        def deal(copy, src, cols, dtype, line, name):
            first = sb_tile([P, cols], dtype, name + "0")
            rest = sb_tile([P, PACK - 1, cols], dtype, name + "r")
            by_t = src.rearrange("p (h l t) -> p h t l", l=line, t=PACK)
            steps = [
                lambda: copy(first[:].rearrange("p (h l) -> p h l", l=line), by_t[:, :, 0, :]),
                lambda: copy(rest[:].rearrange("p t (h l) -> p h t l", l=line), by_t[:, :, 1:PACK, :]),
            ]
            return [first[:]] + [rest[:, t, :] for t in range(PACK - 1)], steps

        w_sd, deal_s = deal(nc.vector.tensor_copy, w_sraw, 2 * P, U8, 16, "w_sd")
        w_d, deal_w = deal(nc.scalar.copy, w_raw[:], P, U16, 8, "w_d")
        w0_d, deal_w0 = deal(nc.scalar.copy, w0_raw[:], P, U32, 4, "w0_d")

        def gather(src, lst, dtype, name, offset):
            tile = reuse.tile([P, J], dtype, name=name, align_bytes=64, offset=offset)
            nc.vector.tensor_copy(tile[:], src[:].indirect(lst[:]))
            return tile

        HJ = J // 2
        sorts = (("xt_gs", U8, xt_s, l1, 0), ("xo_gs", U8, xo_s, l2, 128), ("xt_gw", U32, xt_w, l1, 512), ("xo_gw", U16, xo_w, l2, 256))

        def gather_half(h):
            got = {}
            for name, dtype, src, lst, offset in sorts:
                if h == 0:
                    dst = sb_tile([P, HJ], dtype, name + "0")
                else:
                    dst = reuse.tile([P, HJ], dtype, name=name + "1", align_bytes=64, offset=offset)
                nc.vector.tensor_copy(dst[:], src[:].indirect(lst[:, h * HJ // 16 : (h + 1) * HJ // 16]))
                got[name] = dst
            return got

        def first_stage(t, got, acc):
            nc.tensor.matmul_mx(
                out=acc, lhsT=w_d[t].bitcast(E2M1), lhsT_scale=w_sd[t][:, 0:P],
                rhs=got["xt_gw"][:].bitcast(E4M3), rhs_scale=got["xt_gs"][:], start=True, stop=False,
            )
            nc.tensor.matmul_mx(
                out=acc, lhsT=w0_d[t].bitcast(E5M2), lhsT_scale=w_sd[t][:, P : 2 * P],
                rhs=got["xo_gw"][:].bitcast(E2M1), rhs_scale=got["xo_gs"][:], start=False, stop=True,
            )

        def board_half(h, got):
            acc = psum.tile([P, HJ], F32, name="acc0%d" % h, tag="b0%d" % h)
            first_stage(0, got, acc[:])
            a_sb = sb_tile([P, HJ], F32, "a_sb0%d" % h)
            nc.scalar.copy(a_sb[:], acc[:])
            nc.scalar.activation(pw[0][:].indirect(l3[:, h * HJ // 16 : (h + 1) * HJ // 16]), a_sb[:], ACT.Copy)

        deal_w[0]()
        deal_w0[0]()
        half0 = gather_half(0)
        nc.vector.tensor_copy(w_s[64:P, 0, :].bitcast(I32), w_s[0:64, 1, :].bitcast(I32))
        deal_s[0]()
        board_half(0, half0)
        deal_w[1]()
        deal_w0[1]()
        deal_s[1]()
        half1 = gather_half(1)
        board_half(1, half1)
        for t in range(1, PACK):
            acc = psum.tile([P, J], F32, name="acc%d" % t, tag="b%d" % t)
            first_stage(t, half0, acc[:, 0:HJ])
            first_stage(t, half1, acc[:, HJ:J])
            a_sb = sb_tile([P, J], F32, "a_sb%d" % t)
            nc.vector.tensor_copy(a_sb[:], acc[:])
            nc.vector.tensor_copy(pw[t][:].indirect(l3[:]), a_sb[:])

        x7_gw = gather(xt_w, l7, U32, "x7_gw", 1792)
        x7_gs = gather(xt_s, l7, U8, "x7_gs", 1024)

        HO = O // 2
        ys = [[psum.tile([P, HO], F32, name="y%d_%d" % (h, b), tag=("y0", "y1", "y2", "b00")[2 * h + b]) for b in range(2)] for h in range(2)]
        for h in range(2):
            for b in range(2):
                nc.tensor.matmul_mx(
                    out=ys[h][b][:], lhsT=ws_w[:, b * P : (b + 1) * P].bitcast(E5M2), lhsT_scale=ws_s[:, b * P : (b + 1) * P],
                    rhs=x7_gw[:, h * HO : (h + 1) * HO].bitcast(E4M3), rhs_scale=x7_gs[:, h * HO : (h + 1) * HO],
                    start=True, stop=False,
                )

        HC = C // 2
        pg = [sb_tile([P, C], F32, "pg%d" % t) for t in range(PACK)]
        for t in range(PACK):
            gate = sb_tile([P, C], F32, "gate%d" % t)
            pick = sb_tile([P, C], F32, "pick%d" % t)
            prod = sb_tile([P, C], F32, "prod%d" % t)
            for h in range(2):
                cols = slice(h * HC, (h + 1) * HC)
                lcols = slice(h * HC // 16, (h + 1) * HC // 16)
                nc.scalar.activation(gate[:, cols], pw[t][:].indirect(l5[:, lcols]), ACT.Sigmoid,
                                     bias=bg_t[:, t : t + 1], scale=sg_t[:, t : t + 1])
                nc.scalar.activation(pick[:, cols], pw[t][:].indirect(l4[:, lcols]), ACT.Copy, scale=sa_t[:, t : t + 1])
            for h in range(2):
                cols = slice(h * HC, (h + 1) * HC)
                nc.vector.tensor_tensor(prod[:, cols], pick[:, cols], gate[:, cols], ALU.mult)
            for h in range(2):
                cols = slice(h * HC, (h + 1) * HC)
                nc.vector.tensor_tensor(pg[t][:, cols], pw[t][:, cols], prod[:, cols], ALU.max)

        hid = [sb_tile([P, PACK, HO], F32, "hid%d" % h) for h in range(2)]
        for h in range(2):
            for t in range(PACK):
                lcols = slice(h * HO // 16, (h + 1) * HO // 16)
                nc.scalar.activation(hid[h][:, t, :], pg[t][:].indirect(l6[:, lcols]), ACT.Copy, scale=sb_t[:, t : t + 1])

        woven = [sb_tile([P, HO, PACK], BF16, "woven%d" % h) for h in range(2)]
        hq = [sb_tile([P, HO], U32, "hq%d" % h) for h in range(2)]
        hs = [sb_tile([P, HO], U8, "hs%d" % h) for h in range(2)]
        for h in range(2):
            nc.vector.tensor_copy(
                woven[h][:].rearrange("p (c i) t -> p c t i", i=4),
                hid[h][:].rearrange("p t (c i) -> p c t i", i=4),
            )
        for h in range(2):
            nc.vector.quantize_mx(out=hq[h][:].bitcast(E4M3), scales=hs[h][:], in_=woven[h][:].rearrange("p o t -> p (o t)"))
        out_v = out.rearrange("(b p) o -> p b o", p=P)
        for h in range(2):
            res = sb_tile([P, 2, HO], F32, "res%d" % h)
            for b in range(2):
                nc.tensor.matmul_mx(
                    out=ys[h][b][:], lhsT=wb_w[:, b * P : (b + 1) * P].bitcast(E5M2), lhsT_scale=wb_s[:, b * P : (b + 1) * P],
                    rhs=hq[h][:].bitcast(E4M3), rhs_scale=hs[h][:], start=False, stop=True,
                )
            nc.scalar.copy(res[:, 0, :], ys[h][0][:])
            nc.vector.tensor_copy(res[:, 1, :], ys[h][1][:])
            nc.sync.dma_start(out_v[:, :, h * HO : (h + 1) * HO], res[:])
